import numpy as np
import ml_dtypes


def mxq(x, axis, fmt="e4m3"):
    dtype, down = {"e4m3": (ml_dtypes.float8_e4m3fn, 7), "e5m2": (ml_dtypes.float8_e5m2, 14)}[fmt]
    v = np.moveaxis(np.asarray(x, np.float32).astype(ml_dtypes.bfloat16).astype(np.float64), axis, -1)
    blocks = v.reshape(v.shape[:-1] + (-1, 32))
    amax = np.abs(blocks).max(-1, keepdims=True)
    byte = np.maximum(np.where(amax > 0, np.frexp(amax)[1] - 1 + 127, 0) - down, 1)
    scale = np.exp2(byte - 127.0)
    codes = (blocks / scale).astype(np.float32).astype(dtype).astype(np.float64)
    return np.moveaxis((codes * scale).reshape(v.shape), -1, axis)


WIDE = False


def mx_kscale(k):
    if not WIDE:
        return np.ones(k)
    levels = np.array([10, -10, 5, -5, 0])
    if k % 512:
        return np.exp2(np.random.permutation(np.resize(levels, k // 32))).repeat(32)
    a = np.empty((k // 512, 16))
    for p in range(k // 512):
        a[p, :8] = np.random.permutation(np.resize(levels, 8))
        for g in range(8):
            far = levels[np.abs(levels - a[p, g]) >= 10]
            a[p, g + 8] = far[np.random.randint(len(far))]
    return np.exp2(a.ravel()).repeat(32)


def f64(x):
    return np.asarray(x).astype(np.float64)


def striped(idx):
    return np.tile(np.asarray(idx).reshape(-1, 16).T, (8, 1)).astype(np.uint16)


def unstriped(offs):
    return offs[:16].T.reshape(-1).astype(np.int64)


E2M1 = np.array([0.0, 0.5, 1.0, 1.5, 2.0, 3.0, 4.0, 6.0, -0.0, -0.5, -1.0, -1.5, -2.0, -3.0, -4.0, -6.0])


def pack_weight(w, fmt):
    k, n = w.shape
    w = f64(np.asarray(w, np.float32).astype(ml_dtypes.bfloat16)).reshape(k // 32, 32, n)
    amax = np.abs(w).max(1)
    if fmt == "e4m3":
        byte = np.frexp(amax)[1] - 1 + 127 - 7
    else:
        mant, ex = np.frexp(amax / 6.0)
        byte = np.where(mant > 0.5, ex, ex - 1) + 127
    byte = np.clip(np.where(amax > 0, byte, 1), 1, 254)
    scaled = (w * np.exp2(127.0 - byte)[:, None, :]).reshape(k, n).astype(np.float32)
    by_word = np.ascontiguousarray(scaled.reshape(k // 512, 128, 4, n).transpose(0, 1, 3, 2))
    if fmt == "e4m3":
        words = by_word.astype(ml_dtypes.float8_e4m3fn).view(np.uint8)
    else:
        c = by_word.astype(ml_dtypes.float4_e2m1fn).view(np.uint8) & 0xF
        words = (c[..., 0::2] | (c[..., 1::2] << 4)).reshape(k // 512, 128, 2 * n)
    return np.ascontiguousarray(words), np.ascontiguousarray(byte.astype(np.uint8).reshape(k // 512, 16, n))


def unpack_weight(words, scales, fmt):
    g, _, n = scales.shape
    words = np.ascontiguousarray(words).reshape(g, 128, n, -1)
    if fmt == "e4m3":
        vals = words.view(ml_dtypes.float8_e4m3fn).astype(np.float64)
    else:
        nib = np.empty((g, 128, n, 4), np.uint8)
        nib[..., 0::2] = words & 0xF
        nib[..., 1::2] = words >> 4
        vals = E2M1[nib]
    vals = vals * np.repeat(np.exp2(scales.astype(np.float64) - 127.0), 8, axis=1)[..., None]
    return vals.transpose(0, 1, 3, 2).reshape(g * 512, n)


B, N, T, D, DV, NQ = 1, 512, 1024, 1024, 512, 128


def setup_inputs():
    n = np.random.standard_normal
    idx = np.random.permutation(T)[:B * N]
    s = mx_kscale(D)[:, None]
    u = np.ones(T)
    u[idx] = mx_kscale(B * N)
    r = np.random.uniform(0.5, 2.0, T)
    k = n((D, T)) / s
    v = n((DV, T)) / (u * r)
    kp = pack_weight(k, "e2m1")
    return {
        "qT": (n((B, D, NQ)) * s * (0.60 / np.sqrt(D))).astype(np.float32),
        "k_words": np.ascontiguousarray(kp[0].reshape(D // 1024, 2, 128, T, 2).transpose(0, 2, 3, 1, 4)).reshape(D // 1024, 128, T, 4),
        "k_scales": kp[1],
        "vT": v.astype(np.float32),
        "vs": np.tile(u * r, (128, 1)).astype(np.float32),
        "kb": np.tile(n(T), (128, 1)).astype(np.float32),
        "offs": striped(idx),
    }


def reference(qT, k_words, k_scales, vT, vs, kb, offs):
    idx = unstriped(offs)
    k = unpack_weight(k_words.reshape(D // 1024, 128, T, 2, 2).transpose(0, 3, 1, 2, 4).reshape(D // 512, 128, 2 * T), k_scales, "e2m1")
    v = f64(vT)
    pick = lambda x: x[:, idx].reshape(x.shape[0], B, N).transpose(1, 0, 2)
    q = f64(qT)
    score = mxq(q, 1, "e4m3").transpose(0, 2, 1) @ pick(k)
    score = score + pick(f64(kb))[:, :1, :]
    p = 1.0 / (1.0 + np.exp(-score))
    w = p * pick(f64(vs))[:, :1, :]
    y = mxq(w, 2, "e4m3") @ mxq(pick(v).transpose(0, 2, 1), 1, "e4m3")
    y = y / 16.0
    return y

@@ -1,0 +1,211 @@
+from contextlib import ExitStack
+
+import concourse.mybir as mybir
+from concourse.masks import make_identity
+
+F32 = mybir.dt.float32
+BF16 = mybir.dt.bfloat16
+I32 = mybir.dt.int32
+U32 = mybir.dt.uint32
+U16 = mybir.dt.uint16
+U8 = mybir.dt.uint8
+FP8X4 = mybir.dt.float8_e4m3fn_x4
+FP4X4 = mybir.dt.float4_e2m1fn_x4
+ACT = mybir.ActivationFunctionType
+MULT = mybir.AluOpType.mult
+
+P = 128
+N, T, D, DV, NQ = 512, 1024, 1024, 512, 128
+FLOPS = 2 * NQ * N * D + 2 * NQ * N * DV
+ON_SCALAR = 2
+
+
+def tile_attend_sigmoid_bias_topk_kernel(tc, qT, k_words, k_scales, vT, vs, kb, offs, out):
+    nc = tc.nc
+    with ExitStack() as ctx:
+        keep = ctx.enter_context(tc.tile_pool(name="keep", bufs=1))
+        psum = ctx.enter_context(tc.psum_pool(name="psum", bufs=1))
+
+        offsets = keep.tile([P, N // 16], U16, name="offsets")
+        nc.sync.dma_start(offsets[:], offs)
+
+        scale_pool = keep.tile([P, T], U8, name="scale_pool", tag="late_q", align_bytes=64)
+        nc.vector.memset(scale_pool[:].bitcast(I32), 0)
+        warm_in = keep.tile([P, 1], F32, name="warm_in")
+        nc.vector.memset(warm_in[:], 0.0)
+        for quad in range(4):
+            nc.scalar.dma_start(
+                out=scale_pool[32 * quad : 32 * quad + 8, :].bitcast(I32),
+                in_=k_scales[:, 4 * quad : 4 * quad + 4, :].bitcast(I32),
+            )
+        ident = keep.tile([P, P], F32, name="ident")
+        make_identity(nc, ident[:])
+        warm = keep.tile([P, 1], F32, name="warm")
+        nc.scalar.activation(warm[:], warm_in[:], ACT.Sigmoid)
+
+        bias_pool = keep.tile([P, T], F32, name="bias_pool", tag="late_v3", align_bytes=64)
+        nc.vector.memset(bias_pool[:], 0.0)
+        nc.scalar.dma_start(out=bias_pool[0:1, :], in_=kb[0:1, :])
+        size_pool = keep.tile([P, T], F32, name="size_pool", tag="late_words")
+        nc.vector.memset(size_pool[:], 0.0)
+        nc.scalar.dma_start(out=size_pool[1:2, :], in_=vs[0:1, :])
+        k_plane1 = keep.tile([P, N], U8, name="k_plane1", align_bytes=64)
+        nc.vector.memset(k_plane1[:].bitcast(I32), 0)
+
+        v_pool = [None] * 4
+        for c in range(2):
+            v_pool[c] = keep.tile([P, T], F32, name="v_pool%d" % c)
+            nc.sync.dma_start(out=v_pool[c][:], in_=vT[P * c : P * (c + 1), :])
+        word_pool = keep.tile([P, T], U32, name="word_pool")
+        nc.sync.dma_start(
+            out=word_pool[:].bitcast(I32),
+            in_=k_words[0].rearrange("p t b -> p (t b)").bitcast(I32),
+        )
+
+        scale_g = keep.tile([P, N], U8, name="scale_g", tag="late_v2")
+        nc.vector.tensor_copy(scale_g[:], scale_pool[:].indirect(offsets[:]))
+        k_plane0 = keep.tile([P, N], U8, name="k_plane0", align_bytes=64)
+        nc.vector.tensor_copy(
+            k_plane0[:].rearrange("p (r c i) -> p c r i", r=4, i=16),
+            scale_g[:].rearrange("p (c i r) -> p c r i", r=4, i=16),
+        )
+        nc.gpsimd.dma_start(out=k_plane1[0:100, :].bitcast(I32), in_=k_plane0[4:104, :].bitcast(I32))
+        k_plane = [k_plane0, k_plane1]
+
+        q_raw = keep.tile([P, 2, 4 * NQ], F32, name="q_raw", tag="late_q", align_bytes=64)
+        nc.sync.dma_start(out=q_raw[:], in_=qT[0].rearrange("(g p j) q -> p g (j q)", g=2, j=4))
+        v_pool[2] = keep.tile([P, T], F32, name="v_pool2", tag="late_v2")
+        nc.sync.dma_start(out=v_pool[2][:], in_=vT[2 * P : 3 * P, :])
+
+        bias_g = keep.tile([P, N], F32, name="bias_g")
+        nc.vector.tensor_copy(bias_g[:], bias_pool[:].indirect(offsets[:]))
+        v_pool[3] = keep.tile([P, T], F32, name="v_pool3", tag="late_v3", align_bytes=64)
+        nc.sync.dma_start(out=v_pool[3][:], in_=vT[3 * P : 4 * P, :])
+        size_g = keep.tile([P, N], F32, name="size_g")
+        nc.vector.tensor_copy(size_g[:], size_pool[:].indirect(offsets[:]))
+
+        col_ps = psum.tile([P, 4, P], F32, name="col_ps", tag="bank_a")
+        for r in range(4):
+            nc.tensor.matmul(col_ps[:, r, :], bias_g[:, r:N:4], ident[:], start=True, stop=False, is_transpose=True)
+            nc.tensor.matmul(col_ps[:, r, :], size_g[:, r:N:4], ident[:], start=False, stop=True, is_transpose=True)
+        cols = keep.tile([P, 2, 4], F32, name="cols")
+        nc.scalar.copy(cols[:], col_ps[:, :, 0:2].rearrange("p r k -> p k r"))
+
+        v_g = [None] * 4
+        v_grouped = [
+            keep.tile([P, DV * 2], BF16, name="v_grouped%d" % h, tag=("late_w", "v_grouped1")[h], align_bytes=64)
+            for h in range(2)
+        ]
+        v_codes = [None] * 2
+        v_plane = keep.tile([P, DV], U8, name="v_plane", align_bytes=64)
+
+        def gather_values(c):
+            v_g[c] = keep.tile([P, N], BF16, name="v_g%d" % c, tag=("v_g0", "late_q", "late_g2", "v_g3")[c], align_bytes=64)
+            if c < ON_SCALAR:
+                v_bf = keep.tile([P, T], BF16, name="v_bf%d" % c)
+                nc.scalar.activation(v_bf[:], v_pool[c][:], ACT.Copy)
+                nc.scalar.activation(v_g[c][:], v_bf[:].indirect(offsets[:]), ACT.Copy)
+            else:
+                nc.vector.tensor_copy(v_g[c][:], v_pool[c][:].indirect(offsets[:]))
+
+        def turn_values(c):
+            turned = psum.tile([P, 2, P], F32, name="turned%d" % c, tag=("turned0", "score0", "score1", "turned3")[c])
+            words = v_g[c][:].bitcast(F32)
+            for u in range(2):
+                nc.tensor.transpose(turned[:, u, :], words[:, u : N // 2 : 2], ident[:])
+            nc.scalar.copy(
+                v_grouped[c // 2][:, 4 * P * (c % 2) : 4 * P * (c % 2 + 1)].bitcast(F32).rearrange("p (e u) -> p e u", u=2),
+                turned[:].rearrange("p u e -> p e u"),
+            )
+
+        def quantize_values(h, lo, hi):
+            nc.vector.quantize_mx(
+                out=v_codes[h][:, lo:hi].bitcast(FP8X4),
+                scales=v_plane[:, 2 * P * h + lo : 2 * P * h + hi],
+                in_=v_grouped[h][:, 4 * lo : 4 * hi],
+            )
+
+        gather_values(0)
+        turn_values(0)
+
+        word_g = keep.tile([P, N], U32, name="word_g", tag="late_words")
+        nc.vector.tensor_copy(word_g[:], word_pool[:].indirect(offsets[:]))
+        k_codes = keep.tile([P, 2 * N * 2], U8, name="k_codes", align_bytes=64)
+        nc.vector.tensor_copy(
+            k_codes[:].bitcast(U16).rearrange("p (o r c i) -> p o c r i", o=2, r=4, i=4),
+            word_g[:].bitcast(U16).rearrange("p (c i r o) -> p o c r i", o=2, r=4, i=4),
+        )
+
+        q_grouped = keep.tile([P, 2 * NQ * 4], BF16, name="q_grouped", tag="late_g2", align_bytes=64)
+        nc.scalar.copy(
+            q_grouped[:].rearrange("p (g c i j) -> p g c j i", g=2, i=4, j=4),
+            q_raw[:].rearrange("p g (j c i) -> p g c j i", j=4, i=4),
+        )
+        q_codes = keep.tile([P, 2 * NQ], U32, name="q_codes", align_bytes=64)
+        q_plane = keep.tile([P, 2 * NQ], U8, name="q_plane", align_bytes=64)
+        nc.vector.quantize_mx(out=q_codes[:].bitcast(FP8X4), scales=q_plane[:], in_=q_grouped[:])
+
+        gather_values(1)
+
+        prob = keep.tile([P, 4 * NQ], F32, name="prob")
+        for half in range(2):
+            score = psum.tile([P, 2, NQ], F32, name="score%d" % half, tag="score%d" % half)
+            for rr in range(2):
+                r = 2 * half + rr
+                for o in range(2):
+                    at = (4 * o + r) * 2 * P
+                    nc.tensor.matmul_mx(
+                        out=score[:, rr, :],
+                        lhsT=k_codes[:, at : at + 2 * P].bitcast(FP4X4),
+                        lhsT_scale=k_plane[o][:, P * r : P * (r + 1)],
+                        rhs=q_codes[:, NQ * o : NQ * (o + 1)].bitcast(FP8X4),
+                        rhs_scale=q_plane[:, NQ * o : NQ * (o + 1)],
+                        start=(o == 0),
+                        stop=(o == 1),
+                    )
+            for rr in range(2):
+                r = 2 * half + rr
+                nc.scalar.activation(
+                    prob[:, NQ * r : NQ * (r + 1)], score[:, rr, :], ACT.Sigmoid, bias=cols[:, 0, r : r + 1]
+                )
+
+        turn_values(1)
+        gather_values(2)
+        turn_values(2)
+        gather_values(3)
+        turn_values(3)
+
+        v_codes[0] = keep.tile([P, 2 * P], U32, name="v_codes0", tag="late_v3", align_bytes=64)
+        v_codes[1] = keep.tile([P, 2 * P], U32, name="v_codes1", align_bytes=64)
+        quantize_values(0, 0, 2 * P)
+        w_grouped = keep.tile([P, NQ * 4], BF16, name="w_grouped", tag="late_w", align_bytes=64)
+        nc.vector.tensor_tensor(
+            w_grouped[:].rearrange("p (c i r) -> p c r i", r=4, i=4),
+            prob[:].rearrange("p (r c i) -> p c r i", r=4, i=4),
+            cols[:, 1, :].rearrange("p (c r i) -> p c r i", c=1, i=1).to_broadcast([P, NQ // 4, 4, 4]),
+            MULT,
+        )
+        quantize_values(1, 0, P)
+        w_codes = keep.tile([P, NQ], U32, name="w_codes", align_bytes=64)
+        w_plane = keep.tile([P, NQ], U8, name="w_plane", align_bytes=64)
+        nc.vector.quantize_mx(out=w_codes[:].bitcast(FP8X4), scales=w_plane[:], in_=w_grouped[:])
+        quantize_values(1, P, 2 * P)
+
+        for half in range(2):
+            e = slice(half * DV // 2, (half + 1) * DV // 2)
+            acc = psum.tile([P, DV // 2], F32, name="acc%d" % half, tag=("bank_a", "bank_b")[half])
+            nc.tensor.matmul_mx(
+                out=acc[:],
+                lhsT=w_codes[:].bitcast(FP8X4),
+                lhsT_scale=w_plane[:],
+                rhs=v_codes[half][:].bitcast(FP8X4),
+                rhs_scale=v_plane[:, e],
+                start=True,
+                stop=True,
+            )
+            result = keep.tile([P, DV // 2], F32, name="result%d" % half)
+            if half == 0:
+                nc.scalar.activation(result[:], acc[:], ACT.Copy, scale=1.0 / 16.0)
+            else:
+                nc.vector.tensor_scalar(result[:], acc[:], 1.0 / 16.0, None, MULT)
+            nc.sync.dma_start(out=out[0][:, e], in_=result[:])

@@ -17,195 +17,200 @@ MULT = mybir.AluOpType.mult
 P = 128
 N, T, D, DV, NQ = 512, 1024, 1024, 512, 128
 FLOPS = 2 * NQ * N * D + 2 * NQ * N * DV
-ON_SCALAR = 2
 
 
 def tile_attend_sigmoid_bias_topk_kernel(tc, qT, k_words, k_scales, vT, vs, kb, offs, out):
     nc = tc.nc
     with ExitStack() as ctx:
         keep = ctx.enter_context(tc.tile_pool(name="keep", bufs=1))
+        reuse = ctx.enter_context(tc.tile_pool(name="reuse", bufs=1))
         psum = ctx.enter_context(tc.psum_pool(name="psum", bufs=1))
+
+        def bank(shape, name, index):
+            return psum.tile(shape, F32, name=name, offset=2048 * index)
+
+        def sbuf(shape, dtype, name, tag=None):
+            return keep.tile(shape, dtype, name=name, tag=tag or name, align_bytes=64)
+
+        def placed(shape, dtype, name, offset):
+            return reuse.tile(shape, dtype, name=name, offset=offset, align_bytes=64)
 
         offsets = keep.tile([P, N // 16], U16, name="offsets")
         nc.sync.dma_start(offsets[:], offs)
 
-        scale_pool = keep.tile([P, T], U8, name="scale_pool", tag="late_q", align_bytes=64)
-        nc.vector.memset(scale_pool[:].bitcast(I32), 0)
-        warm_in = keep.tile([P, 1], F32, name="warm_in")
+        warm_in = sbuf([P, 1], F32, "warm_in")
         nc.vector.memset(warm_in[:], 0.0)
+        warm = sbuf([P, 1], F32, "warm")
+        nc.scalar.activation(warm[:], warm_in[:], ACT.Sigmoid)
+
+        first = [sbuf([P, T // 2], F32, "first%d" % h) for h in range(2)]
+        nc.sync.dma_start(out=first[0][:], in_=vT[0:P, 0 : T // 2])
+        bias_pool = sbuf([P, T], F32, "bias_pool")
+        nc.vector.memset(bias_pool[:], 0.0)
+        nc.sync.dma_start(out=bias_pool[0:1, :], in_=kb[0:1, :])
+        nc.sync.dma_start(out=first[1][:], in_=vT[0:P, T // 2 : T])
+        scale_pool = sbuf([P, T], U8, "scale_pool")
+        nc.vector.memset(scale_pool[:].bitcast(I32), 0)
         for quad in range(4):
-            nc.scalar.dma_start(
+            nc.sync.dma_start(
                 out=scale_pool[32 * quad : 32 * quad + 8, :].bitcast(I32),
                 in_=k_scales[:, 4 * quad : 4 * quad + 4, :].bitcast(I32),
             )
-        ident = keep.tile([P, P], F32, name="ident")
+        ident = sbuf([P, P], F32, "ident")
         make_identity(nc, ident[:])
-        warm = keep.tile([P, 1], F32, name="warm")
-        nc.scalar.activation(warm[:], warm_in[:], ACT.Sigmoid)
-
-        bias_pool = keep.tile([P, T], F32, name="bias_pool", tag="late_v3", align_bytes=64)
-        nc.vector.memset(bias_pool[:], 0.0)
-        nc.scalar.dma_start(out=bias_pool[0:1, :], in_=kb[0:1, :])
-        size_pool = keep.tile([P, T], F32, name="size_pool", tag="late_words")
+        size_pool = sbuf([P, T], F32, "size_pool")
         nc.vector.memset(size_pool[:], 0.0)
-        nc.scalar.dma_start(out=size_pool[1:2, :], in_=vs[0:1, :])
-        k_plane1 = keep.tile([P, N], U8, name="k_plane1", align_bytes=64)
+        k_plane1 = sbuf([P, N], U8, "k_plane1")
         nc.vector.memset(k_plane1[:].bitcast(I32), 0)
 
-        v_pool = [None] * 4
-        for c in range(2):
-            v_pool[c] = keep.tile([P, T], F32, name="v_pool%d" % c)
+        v_pool = [None, placed([P, T], F32, "v_pool1", 4096), sbuf([P, T], F32, "v_pool2"), placed([P, T], F32, "v_pool3", 0)]
+
+        def load_values(c):
             nc.sync.dma_start(out=v_pool[c][:], in_=vT[P * c : P * (c + 1), :])
-        word_pool = keep.tile([P, T], U32, name="word_pool")
+
+        load_values(1)
+        word_pool = sbuf([P, T], U32, "word_pool")
         nc.sync.dma_start(
             out=word_pool[:].bitcast(I32),
             in_=k_words[0].rearrange("p t b -> p (t b)").bitcast(I32),
         )
+        q_raw = sbuf([P, 2, 4 * NQ], F32, "q_raw", "after_q")
+        nc.sync.dma_start(out=q_raw[:], in_=qT[0].rearrange("(g p j) q -> p g (j q)", g=2, j=4))
 
-        scale_g = keep.tile([P, N], U8, name="scale_g", tag="late_v2")
+        load_values(2)
+        nc.sync.dma_start(out=size_pool[0:1, :], in_=vs[0:1, :])
+        load_values(3)
+
+        def columns(name, pool, index):
+            listed = sbuf([P, N], F32, name + "_g")
+            nc.vector.tensor_copy(listed[:], pool[:].indirect(offsets[:]))
+            turned = bank([P, 4, P], name + "_ps", index)
+            for r in range(4):
+                nc.tensor.transpose(turned[:, r, :], listed[:, r:N:4], ident[:])
+            return turned
+
+        v_g = [None] * 4
+        v_grouped = [None] * 4
+        v_codes = sbuf([P, DV], U32, "v_codes")
+        v_plane = sbuf([P, DV], U8, "v_plane")
+
+        def gather_on_scalar(c, v_bf, tile):
+            v_g[c] = tile
+            nc.scalar.activation(v_g[c][:], v_bf[:].indirect(offsets[:]), ACT.Copy)
+
+        def turn_values(c, index, copy, grouped):
+            v_grouped[c] = grouped
+            turned = bank([P, 2, P], "turned%d" % c, index)
+            words = v_g[c][:].bitcast(F32)
+            for u in range(2):
+                nc.tensor.transpose(turned[:, u, :], words[:, u : N // 2 : 2], ident[:])
+            copy(grouped[:].bitcast(F32).rearrange("p (e u) -> p e u", u=2), turned[:].rearrange("p u e -> p e u"))
+
+        def quantize_values(c):
+            nc.vector.quantize_mx(
+                out=v_codes[:, P * c : P * (c + 1)].bitcast(FP8X4),
+                scales=v_plane[:, P * c : P * (c + 1)],
+                in_=v_grouped[c][:],
+            )
+
+        v_bf0 = sbuf([P, T], BF16, "v_bf0")
+        for h in range(2):
+            nc.scalar.activation(v_bf0[:, h * T // 2 : (h + 1) * T // 2], first[h][:], ACT.Copy)
+        gather_on_scalar(0, v_bf0, sbuf([P, N], BF16, "v_g0"))
+        v_bf1 = sbuf([P, T], BF16, "v_bf1", "after_gather1")
+        nc.scalar.activation(v_bf1[:], v_pool[1][:], ACT.Copy)
+        bias_turned = columns("bias", bias_pool, 4)
+        bias_col = placed([P, 4], F32, "bias_col", 4096 + 1024)
+        nc.scalar.copy(bias_col[:], bias_turned[:, :, 0])
+        turn_values(0, 5, nc.scalar.copy, placed([P, 4 * P], BF16, "v_grouped0", 4096))
+
+        scale_g = sbuf([P, N], U8, "scale_g")
         nc.vector.tensor_copy(scale_g[:], scale_pool[:].indirect(offsets[:]))
-        k_plane0 = keep.tile([P, N], U8, name="k_plane0", align_bytes=64)
+        k_plane0 = sbuf([P, N], U8, "k_plane0")
         nc.vector.tensor_copy(
             k_plane0[:].rearrange("p (r c i) -> p c r i", r=4, i=16),
             scale_g[:].rearrange("p (c i r) -> p c r i", r=4, i=16),
         )
-        nc.gpsimd.dma_start(out=k_plane1[0:100, :].bitcast(I32), in_=k_plane0[4:104, :].bitcast(I32))
+        nc.sync.dma_start(out=k_plane1[0:100, :].bitcast(I32), in_=k_plane0[4:104, :].bitcast(I32))
         k_plane = [k_plane0, k_plane1]
 
-        q_raw = keep.tile([P, 2, 4 * NQ], F32, name="q_raw", tag="late_q", align_bytes=64)
-        nc.sync.dma_start(out=q_raw[:], in_=qT[0].rearrange("(g p j) q -> p g (j q)", g=2, j=4))
-        v_pool[2] = keep.tile([P, T], F32, name="v_pool2", tag="late_v2")
-        nc.sync.dma_start(out=v_pool[2][:], in_=vT[2 * P : 3 * P, :])
-
-        bias_g = keep.tile([P, N], F32, name="bias_g")
-        nc.vector.tensor_copy(bias_g[:], bias_pool[:].indirect(offsets[:]))
-        v_pool[3] = keep.tile([P, T], F32, name="v_pool3", tag="late_v3", align_bytes=64)
-        nc.sync.dma_start(out=v_pool[3][:], in_=vT[3 * P : 4 * P, :])
-        size_g = keep.tile([P, N], F32, name="size_g")
-        nc.vector.tensor_copy(size_g[:], size_pool[:].indirect(offsets[:]))
-
-        col_ps = psum.tile([P, 4, P], F32, name="col_ps", tag="bank_a")
-        for r in range(4):
-            nc.tensor.matmul(col_ps[:, r, :], bias_g[:, r:N:4], ident[:], start=True, stop=False, is_transpose=True)
-            nc.tensor.matmul(col_ps[:, r, :], size_g[:, r:N:4], ident[:], start=False, stop=True, is_transpose=True)
-        cols = keep.tile([P, 2, 4], F32, name="cols")
-        nc.scalar.copy(cols[:], col_ps[:, :, 0:2].rearrange("p r k -> p k r"))
-
-        v_g = [None] * 4
-        v_grouped = [
-            keep.tile([P, DV * 2], BF16, name="v_grouped%d" % h, tag=("late_w", "v_grouped1")[h], align_bytes=64)
-            for h in range(2)
-        ]
-        v_codes = [None] * 2
-        v_plane = keep.tile([P, DV], U8, name="v_plane", align_bytes=64)
-
-        def gather_values(c):
-            v_g[c] = keep.tile([P, N], BF16, name="v_g%d" % c, tag=("v_g0", "late_q", "late_g2", "v_g3")[c], align_bytes=64)
-            if c < ON_SCALAR:
-                v_bf = keep.tile([P, T], BF16, name="v_bf%d" % c)
-                nc.scalar.activation(v_bf[:], v_pool[c][:], ACT.Copy)
-                nc.scalar.activation(v_g[c][:], v_bf[:].indirect(offsets[:]), ACT.Copy)
-            else:
-                nc.vector.tensor_copy(v_g[c][:], v_pool[c][:].indirect(offsets[:]))
-
-        def turn_values(c):
-            turned = psum.tile([P, 2, P], F32, name="turned%d" % c, tag=("turned0", "score0", "score1", "turned3")[c])
-            words = v_g[c][:].bitcast(F32)
-            for u in range(2):
-                nc.tensor.transpose(turned[:, u, :], words[:, u : N // 2 : 2], ident[:])
-            nc.scalar.copy(
-                v_grouped[c // 2][:, 4 * P * (c % 2) : 4 * P * (c % 2 + 1)].bitcast(F32).rearrange("p (e u) -> p e u", u=2),
-                turned[:].rearrange("p u e -> p e u"),
-            )
-
-        def quantize_values(h, lo, hi):
-            nc.vector.quantize_mx(
-                out=v_codes[h][:, lo:hi].bitcast(FP8X4),
-                scales=v_plane[:, 2 * P * h + lo : 2 * P * h + hi],
-                in_=v_grouped[h][:, 4 * lo : 4 * hi],
-            )
-
-        gather_values(0)
-        turn_values(0)
-
-        word_g = keep.tile([P, N], U32, name="word_g", tag="late_words")
+        word_g = sbuf([P, N], U32, "word_g")
         nc.vector.tensor_copy(word_g[:], word_pool[:].indirect(offsets[:]))
-        k_codes = keep.tile([P, 2 * N * 2], U8, name="k_codes", align_bytes=64)
+        k_codes = sbuf([P, 2 * N * 2], U8, "k_codes")
         nc.vector.tensor_copy(
             k_codes[:].bitcast(U16).rearrange("p (o r c i) -> p o c r i", o=2, r=4, i=4),
             word_g[:].bitcast(U16).rearrange("p (c i r o) -> p o c r i", o=2, r=4, i=4),
         )
 
-        q_grouped = keep.tile([P, 2 * NQ * 4], BF16, name="q_grouped", tag="late_g2", align_bytes=64)
+        q_grouped = sbuf([P, 2 * NQ * 4], BF16, "q_grouped", "after_q_codes")
         nc.scalar.copy(
             q_grouped[:].rearrange("p (g c i j) -> p g c j i", g=2, i=4, j=4),
             q_raw[:].rearrange("p g (j c i) -> p g c j i", j=4, i=4),
         )
-        q_codes = keep.tile([P, 2 * NQ], U32, name="q_codes", align_bytes=64)
-        q_plane = keep.tile([P, 2 * NQ], U8, name="q_plane", align_bytes=64)
+        q_codes = sbuf([P, 2 * NQ], U32, "q_codes")
+        q_plane = sbuf([P, 2 * NQ], U8, "q_plane")
         nc.vector.quantize_mx(out=q_codes[:].bitcast(FP8X4), scales=q_plane[:], in_=q_grouped[:])
+        quantize_values(0)
 
-        gather_values(1)
+        gather_on_scalar(1, v_bf1, sbuf([P, N], BF16, "v_g1", "after_q"))
 
-        prob = keep.tile([P, 4 * NQ], F32, name="prob")
-        for half in range(2):
-            score = psum.tile([P, 2, NQ], F32, name="score%d" % half, tag="score%d" % half)
-            for rr in range(2):
-                r = 2 * half + rr
-                for o in range(2):
-                    at = (4 * o + r) * 2 * P
-                    nc.tensor.matmul_mx(
-                        out=score[:, rr, :],
-                        lhsT=k_codes[:, at : at + 2 * P].bitcast(FP4X4),
-                        lhsT_scale=k_plane[o][:, P * r : P * (r + 1)],
-                        rhs=q_codes[:, NQ * o : NQ * (o + 1)].bitcast(FP8X4),
-                        rhs_scale=q_plane[:, NQ * o : NQ * (o + 1)],
-                        start=(o == 0),
-                        stop=(o == 1),
-                    )
-            for rr in range(2):
-                r = 2 * half + rr
-                nc.scalar.activation(
-                    prob[:, NQ * r : NQ * (r + 1)], score[:, rr, :], ACT.Sigmoid, bias=cols[:, 0, r : r + 1]
+        score = [bank([P, NQ], "score%d" % r, r) for r in range(4)]
+        for o in range(2):
+            for r in range(4):
+                at = (4 * o + r) * 2 * P
+                nc.tensor.matmul_mx(
+                    out=score[r][:],
+                    lhsT=k_codes[:, at : at + 2 * P].bitcast(FP4X4),
+                    lhsT_scale=k_plane[o][:, P * r : P * (r + 1)],
+                    rhs=q_codes[:, NQ * o : NQ * (o + 1)].bitcast(FP8X4),
+                    rhs_scale=q_plane[:, NQ * o : NQ * (o + 1)],
+                    start=(o == 0),
+                    stop=(o == 1),
                 )
+        prob = sbuf([P, 4 * NQ], F32, "prob", "after_gather1")
+        for r in range(4):
+            nc.scalar.activation(
+                prob[:, NQ * r : NQ * (r + 1)], score[r][:], ACT.Sigmoid, bias=bias_col[:, r : r + 1]
+            )
 
-        turn_values(1)
-        gather_values(2)
-        turn_values(2)
-        gather_values(3)
-        turn_values(3)
+        size_turned = columns("size", size_pool, 0)
+        v_bf2 = sbuf([P, T], BF16, "v_bf2", "after_q_codes")
+        nc.vector.tensor_copy(v_bf2[:], v_pool[2][:])
+        gather_on_scalar(2, v_bf2, placed([P, N], BF16, "v_g2", 4096 + 1024))
+        v_g[3] = sbuf([P, N], BF16, "v_g3")
+        nc.vector.tensor_copy(v_g[3][:], v_pool[3][:].indirect(offsets[:]))
 
-        v_codes[0] = keep.tile([P, 2 * P], U32, name="v_codes0", tag="late_v3", align_bytes=64)
-        v_codes[1] = keep.tile([P, 2 * P], U32, name="v_codes1", align_bytes=64)
-        quantize_values(0, 0, 2 * P)
-        w_grouped = keep.tile([P, NQ * 4], BF16, name="w_grouped", tag="late_w", align_bytes=64)
+        w_grouped = placed([P, NQ * 4], BF16, "w_grouped", 0)
         nc.vector.tensor_tensor(
             w_grouped[:].rearrange("p (c i r) -> p c r i", r=4, i=4),
             prob[:].rearrange("p (r c i) -> p c r i", r=4, i=4),
-            cols[:, 1, :].rearrange("p (c r i) -> p c r i", c=1, i=1).to_broadcast([P, NQ // 4, 4, 4]),
+            size_turned[:, :, 0:1].rearrange("p r (c i) -> p c r i", c=1).to_broadcast([P, NQ // 4, 4, 4]),
             MULT,
         )
-        quantize_values(1, 0, P)
-        w_codes = keep.tile([P, NQ], U32, name="w_codes", align_bytes=64)
-        w_plane = keep.tile([P, NQ], U8, name="w_plane", align_bytes=64)
+        turn_values(1, 1, nc.vector.tensor_copy, placed([P, 4 * P], BF16, "v_grouped1", 1024))
+        w_codes = sbuf([P, NQ], U32, "w_codes")
+        w_plane = sbuf([P, NQ], U8, "w_plane")
         nc.vector.quantize_mx(out=w_codes[:].bitcast(FP8X4), scales=w_plane[:], in_=w_grouped[:])
-        quantize_values(1, P, 2 * P)
+        quantize_values(1)
+        turn_values(3, 2, nc.scalar.copy, sbuf([P, 4 * P], BF16, "v_grouped3"))
+        quantize_values(3)
+        turn_values(2, 3, nc.scalar.copy, sbuf([P, 4 * P], BF16, "v_grouped2"))
+        quantize_values(2)
 
-        for half in range(2):
-            e = slice(half * DV // 2, (half + 1) * DV // 2)
-            acc = psum.tile([P, DV // 2], F32, name="acc%d" % half, tag=("bank_a", "bank_b")[half])
+        for name, lo, hi, index in (("a", 0, 2 * P, 6), ("b", 3 * P, 4 * P, 7), ("c", 2 * P, 3 * P, 4)):
+            acc = bank([P, hi - lo], "acc_" + name, index)
             nc.tensor.matmul_mx(
                 out=acc[:],
                 lhsT=w_codes[:].bitcast(FP8X4),
                 lhsT_scale=w_plane[:],
-                rhs=v_codes[half][:].bitcast(FP8X4),
-                rhs_scale=v_plane[:, e],
+                rhs=v_codes[:, lo:hi].bitcast(FP8X4),
+                rhs_scale=v_plane[:, lo:hi],
                 start=True,
                 stop=True,
             )
-            result = keep.tile([P, DV // 2], F32, name="result%d" % half)
-            if half == 0:
+            result = sbuf([P, hi - lo], F32, "result_" + name)
+            if name != "c":
                 nc.scalar.activation(result[:], acc[:], ACT.Copy, scale=1.0 / 16.0)
             else:
                 nc.vector.tensor_scalar(result[:], acc[:], 1.0 / 16.0, None, MULT)
-            nc.sync.dma_start(out=out[0][:, e], in_=result[:])
+            nc.sync.dma_start(out=out[0][:, lo:hi], in_=result[:])

from contextlib import ExitStack

import concourse.mybir as mybir
from concourse.masks import make_identity

F32 = mybir.dt.float32
BF16 = mybir.dt.bfloat16
I32 = mybir.dt.int32
U32 = mybir.dt.uint32
U16 = mybir.dt.uint16
U8 = mybir.dt.uint8
FP8X4 = mybir.dt.float8_e4m3fn_x4
FP4X4 = mybir.dt.float4_e2m1fn_x4
ACT = mybir.ActivationFunctionType
MULT = mybir.AluOpType.mult

P = 128
N, T, D, DV, NQ = 512, 1024, 1024, 512, 128
FLOPS = 2 * NQ * N * D + 2 * NQ * N * DV


def tile_attend_sigmoid_bias_topk_kernel(tc, qT, k_words, k_scales, vT, vs, kb, offs, out):
    nc = tc.nc
    with ExitStack() as ctx:
        keep = ctx.enter_context(tc.tile_pool(name="keep", bufs=1))
        reuse = ctx.enter_context(tc.tile_pool(name="reuse", bufs=1))
        psum = ctx.enter_context(tc.psum_pool(name="psum", bufs=1))

        def bank(shape, name, index):
            return psum.tile(shape, F32, name=name, offset=2048 * index)

        def sbuf(shape, dtype, name, tag=None):
            return keep.tile(shape, dtype, name=name, tag=tag or name, align_bytes=64)

        def placed(shape, dtype, name, offset):
            return reuse.tile(shape, dtype, name=name, offset=offset, align_bytes=64)

        offsets = keep.tile([P, N // 16], U16, name="offsets")
        nc.sync.dma_start(offsets[:], offs)

        warm_in = sbuf([P, 1], F32, "warm_in")
        nc.vector.memset(warm_in[:], 0.0)
        warm = sbuf([P, 1], F32, "warm")
        nc.scalar.activation(warm[:], warm_in[:], ACT.Sigmoid)

        first = [sbuf([P, T // 2], F32, "first%d" % h) for h in range(2)]
        nc.sync.dma_start(out=first[0][:], in_=vT[0:P, 0 : T // 2])
        bias_pool = sbuf([P, T], F32, "bias_pool")
        nc.vector.memset(bias_pool[:], 0.0)
        nc.sync.dma_start(out=bias_pool[0:1, :], in_=kb[0:1, :])
        nc.sync.dma_start(out=first[1][:], in_=vT[0:P, T // 2 : T])
        scale_pool = sbuf([P, T], U8, "scale_pool")
        nc.vector.memset(scale_pool[:].bitcast(I32), 0)
        for quad in range(4):
            nc.sync.dma_start(
                out=scale_pool[32 * quad : 32 * quad + 8, :].bitcast(I32),
                in_=k_scales[:, 4 * quad : 4 * quad + 4, :].bitcast(I32),
            )
        ident = sbuf([P, P], F32, "ident")
        make_identity(nc, ident[:])
        size_pool = sbuf([P, T], F32, "size_pool")
        nc.vector.memset(size_pool[:], 0.0)
        k_plane1 = sbuf([P, N], U8, "k_plane1")
        nc.vector.memset(k_plane1[:].bitcast(I32), 0)

        v_pool = [None, placed([P, T], F32, "v_pool1", 4096), sbuf([P, T], F32, "v_pool2"), placed([P, T], F32, "v_pool3", 0)]

        def load_values(c):
            nc.sync.dma_start(out=v_pool[c][:], in_=vT[P * c : P * (c + 1), :])

        load_values(1)
        word_pool = sbuf([P, T], U32, "word_pool")
        nc.sync.dma_start(
            out=word_pool[:].bitcast(I32),
            in_=k_words[0].rearrange("p t b -> p (t b)").bitcast(I32),
        )
        q_raw = sbuf([P, 2, 4 * NQ], F32, "q_raw", "after_q")
        nc.sync.dma_start(out=q_raw[:], in_=qT[0].rearrange("(g p j) q -> p g (j q)", g=2, j=4))

        load_values(2)
        nc.sync.dma_start(out=size_pool[0:1, :], in_=vs[0:1, :])
        load_values(3)

        def columns(name, pool, index):
            listed = sbuf([P, N], F32, name + "_g")
            nc.vector.tensor_copy(listed[:], pool[:].indirect(offsets[:]))
            turned = bank([P, 4, P], name + "_ps", index)
            for r in range(4):
                nc.tensor.transpose(turned[:, r, :], listed[:, r:N:4], ident[:])
            return turned

        v_g = [None] * 4
        v_grouped = [None] * 4
        v_codes = sbuf([P, DV], U32, "v_codes")
        v_plane = sbuf([P, DV], U8, "v_plane")

        def gather_on_scalar(c, v_bf, tile):
            v_g[c] = tile
            nc.scalar.activation(v_g[c][:], v_bf[:].indirect(offsets[:]), ACT.Copy)

        def turn_values(c, index, copy, grouped):
            v_grouped[c] = grouped
            turned = bank([P, 2, P], "turned%d" % c, index)
            words = v_g[c][:].bitcast(F32)
            for u in range(2):
                nc.tensor.transpose(turned[:, u, :], words[:, u : N // 2 : 2], ident[:])
            copy(grouped[:].bitcast(F32).rearrange("p (e u) -> p e u", u=2), turned[:].rearrange("p u e -> p e u"))

        def quantize_values(c):
            nc.vector.quantize_mx(
                out=v_codes[:, P * c : P * (c + 1)].bitcast(FP8X4),
                scales=v_plane[:, P * c : P * (c + 1)],
                in_=v_grouped[c][:],
            )

        v_bf0 = sbuf([P, T], BF16, "v_bf0")
        for h in range(2):
            nc.scalar.activation(v_bf0[:, h * T // 2 : (h + 1) * T // 2], first[h][:], ACT.Copy)
        gather_on_scalar(0, v_bf0, sbuf([P, N], BF16, "v_g0"))
        v_bf1 = sbuf([P, T], BF16, "v_bf1", "after_gather1")
        nc.scalar.activation(v_bf1[:], v_pool[1][:], ACT.Copy)
        bias_turned = columns("bias", bias_pool, 4)
        bias_col = placed([P, 4], F32, "bias_col", 4096 + 1024)
        nc.scalar.copy(bias_col[:], bias_turned[:, :, 0])
        turn_values(0, 5, nc.scalar.copy, placed([P, 4 * P], BF16, "v_grouped0", 4096))

        scale_g = sbuf([P, N], U8, "scale_g")
        nc.vector.tensor_copy(scale_g[:], scale_pool[:].indirect(offsets[:]))
        k_plane0 = sbuf([P, N], U8, "k_plane0")
        nc.vector.tensor_copy(
            k_plane0[:].rearrange("p (r c i) -> p c r i", r=4, i=16),
            scale_g[:].rearrange("p (c i r) -> p c r i", r=4, i=16),
        )
        nc.sync.dma_start(out=k_plane1[0:100, :].bitcast(I32), in_=k_plane0[4:104, :].bitcast(I32))
        k_plane = [k_plane0, k_plane1]

        word_g = sbuf([P, N], U32, "word_g")
        nc.vector.tensor_copy(word_g[:], word_pool[:].indirect(offsets[:]))
        k_codes = sbuf([P, 2 * N * 2], U8, "k_codes")
        nc.vector.tensor_copy(
            k_codes[:].bitcast(U16).rearrange("p (o r c i) -> p o c r i", o=2, r=4, i=4),
            word_g[:].bitcast(U16).rearrange("p (c i r o) -> p o c r i", o=2, r=4, i=4),
        )

        q_grouped = sbuf([P, 2 * NQ * 4], BF16, "q_grouped", "after_q_codes")
        nc.scalar.copy(
            q_grouped[:].rearrange("p (g c i j) -> p g c j i", g=2, i=4, j=4),
            q_raw[:].rearrange("p g (j c i) -> p g c j i", j=4, i=4),
        )
        q_codes = sbuf([P, 2 * NQ], U32, "q_codes")
        q_plane = sbuf([P, 2 * NQ], U8, "q_plane")
        nc.vector.quantize_mx(out=q_codes[:].bitcast(FP8X4), scales=q_plane[:], in_=q_grouped[:])
        quantize_values(0)

        gather_on_scalar(1, v_bf1, sbuf([P, N], BF16, "v_g1", "after_q"))

        score = [bank([P, NQ], "score%d" % r, r) for r in range(4)]
        for o in range(2):
            for r in range(4):
                at = (4 * o + r) * 2 * P
                nc.tensor.matmul_mx(
                    out=score[r][:],
                    lhsT=k_codes[:, at : at + 2 * P].bitcast(FP4X4),
                    lhsT_scale=k_plane[o][:, P * r : P * (r + 1)],
                    rhs=q_codes[:, NQ * o : NQ * (o + 1)].bitcast(FP8X4),
                    rhs_scale=q_plane[:, NQ * o : NQ * (o + 1)],
                    start=(o == 0),
                    stop=(o == 1),
                )
        prob = sbuf([P, 4 * NQ], F32, "prob", "after_gather1")
        for r in range(4):
            nc.scalar.activation(
                prob[:, NQ * r : NQ * (r + 1)], score[r][:], ACT.Sigmoid, bias=bias_col[:, r : r + 1]
            )

        size_turned = columns("size", size_pool, 0)
        v_bf2 = sbuf([P, T], BF16, "v_bf2", "after_q_codes")
        nc.vector.tensor_copy(v_bf2[:], v_pool[2][:])
        gather_on_scalar(2, v_bf2, placed([P, N], BF16, "v_g2", 4096 + 1024))
        v_g[3] = sbuf([P, N], BF16, "v_g3")
        nc.vector.tensor_copy(v_g[3][:], v_pool[3][:].indirect(offsets[:]))

        w_grouped = placed([P, NQ * 4], BF16, "w_grouped", 0)
        nc.vector.tensor_tensor(
            w_grouped[:].rearrange("p (c i r) -> p c r i", r=4, i=4),
            prob[:].rearrange("p (r c i) -> p c r i", r=4, i=4),
            size_turned[:, :, 0:1].rearrange("p r (c i) -> p c r i", c=1).to_broadcast([P, NQ // 4, 4, 4]),
            MULT,
        )
        turn_values(1, 1, nc.vector.tensor_copy, placed([P, 4 * P], BF16, "v_grouped1", 1024))
        w_codes = sbuf([P, NQ], U32, "w_codes")
        w_plane = sbuf([P, NQ], U8, "w_plane")
        nc.vector.quantize_mx(out=w_codes[:].bitcast(FP8X4), scales=w_plane[:], in_=w_grouped[:])
        quantize_values(1)
        turn_values(3, 2, nc.scalar.copy, sbuf([P, 4 * P], BF16, "v_grouped3"))
        quantize_values(3)
        turn_values(2, 3, nc.scalar.copy, sbuf([P, 4 * P], BF16, "v_grouped2"))
        quantize_values(2)

        for name, lo, hi, index in (("a", 0, 2 * P, 6), ("b", 3 * P, 4 * P, 7), ("c", 2 * P, 3 * P, 4)):
            acc = bank([P, hi - lo], "acc_" + name, index)
            nc.tensor.matmul_mx(
                out=acc[:],
                lhsT=w_codes[:].bitcast(FP8X4),
                lhsT_scale=w_plane[:],
                rhs=v_codes[:, lo:hi].bitcast(FP8X4),
                rhs_scale=v_plane[:, lo:hi],
                start=True,
                stop=True,
            )
            result = sbuf([P, hi - lo], F32, "result_" + name)
            if name != "c":
                nc.scalar.activation(result[:], acc[:], ACT.Copy, scale=1.0 / 16.0)
            else:
                nc.vector.tensor_scalar(result[:], acc[:], 1.0 / 16.0, None, MULT)
            nc.sync.dma_start(out=out[0][:, lo:hi], in_=result[:])
